import numpy as np
import ml_dtypes


def mxq(x, axis, fmt="e4m3"):
    dtype, down = {"e4m3": (ml_dtypes.float8_e4m3fn, 7), "e5m2": (ml_dtypes.float8_e5m2, 14)}[fmt]
    v = np.moveaxis(np.asarray(x, np.float32).astype(ml_dtypes.bfloat16).astype(np.float64), axis, -1)
    blocks = v.reshape(v.shape[:-1] + (-1, 32))
    amax = np.abs(blocks).max(-1, keepdims=True)
    byte = np.maximum(np.where(amax > 0, np.frexp(amax)[1] - 1 + 127, 0) - down, 1)
    scale = np.exp2(byte - 127.0)
    codes = (blocks / scale).astype(np.float32).astype(dtype).astype(np.float64)
    return np.moveaxis((codes * scale).reshape(v.shape), -1, axis)


WIDE = False


def mx_kscale(k):
    if not WIDE:
        return np.ones(k)
    levels = np.array([10, -10, 5, -5, 0])
    if k % 512:
        return np.exp2(np.random.permutation(np.resize(levels, k // 32))).repeat(32)
    a = np.empty((k // 512, 16))
    for p in range(k // 512):
        a[p, :8] = np.random.permutation(np.resize(levels, 8))
        for g in range(8):
            far = levels[np.abs(levels - a[p, g]) >= 10]
            a[p, g + 8] = far[np.random.randint(len(far))]
    return np.exp2(a.ravel()).repeat(32)


def f64(x):
    return np.asarray(x).astype(np.float64)


def striped(idx):
    return np.tile(idx.reshape(-1, 16).T, (8, 1)).astype(np.uint16)


def unstriped(offs):
    return offs[:16].T.reshape(-1).astype(np.int64)


def gelu(v):
    return 0.5 * v * (1.0 + np.tanh(np.sqrt(2.0 / np.pi) * (v + 0.044715 * v**3)))


K, T, E, C, N = 1024, 1024, 16, 128, 256


def by_expert(wq, xq):
    return np.concatenate([wq[e].T @ xq[:, e * C:(e + 1) * C] for e in range(E)], axis=1)


def setup_inputs():
    n = np.random.standard_normal
    s = mx_kscale(K)[:, None]
    first = np.random.permutation(np.repeat(np.arange(E), T // E))
    second = (first + 1 + np.random.permutation(np.repeat(np.arange(E - 1), -(-T // (E - 1)))[:T])) % E
    while np.bincount(second, minlength=E).max() != T // E:
        load = np.bincount(second, minlength=E); hi, lo = int(load.argmax()), int(load.argmin())
        t = np.flatnonzero((second == hi) & (first != lo))[0]; second[t] = lo
    slot_token = np.empty(E * C, np.int64); pos = np.empty((2, T), np.int64); fill = np.zeros(E, np.int64)
    place = np.stack([np.random.permutation(C) for _ in range(E)])
    for r, deal in enumerate((first, second)):
        for t in np.random.permutation(T):
            e = deal[t]; j = e * C + place[e, fill[e]]; fill[e] += 1; slot_token[j] = t; pos[r, t] = j
    g = np.random.uniform(0.2, 0.8, T)
    return {
        "xT": (n((K, T)) * s).astype(np.float32),
        "w": (n((E, K, N)) / np.sqrt(K) / s[None]).astype(np.float32),
        "b": (0.3 * n((N, E))).astype(np.float32),
        "gate": np.stack([np.tile(g, (N, 1)), np.tile(1.0 - g, (N, 1))]).astype(np.float32),
        "offs": striped(slot_token),
        "pos1": striped(pos[0]),
        "pos2": striped(pos[1]),
    }


def reference(xT, w, b, gate, offs, pos1, pos2):
    idx = unstriped(offs)
    xq = mxq(f64(xT)[:, idx], 0, "e4m3")
    y = by_expert(mxq(f64(w), 1, "e4m3"), xq)
    y = gelu(y + np.repeat(f64(b), C, axis=1))
    return f64(gate[0]) * y[:, unstriped(pos1)] + f64(gate[1]) * y[:, unstriped(pos2)]

@@ -1,0 +1,177 @@
+from contextlib import ExitStack
+
+import concourse.mybir as mybir
+
+K, T, E, C, N = 1024, 1024, 16, 128, 256
+FLOPS = 2 * K * N * E * C
+
+F32 = mybir.dt.float32
+BF16 = mybir.dt.bfloat16
+U32 = mybir.dt.uint32
+U16 = mybir.dt.uint16
+U8 = mybir.dt.uint8
+FP8X4 = mybir.dt.float8_e4m3fn_x4
+MULT = mybir.AluOpType.mult
+ADD = mybir.AluOpType.add
+GELU = mybir.ActivationFunctionType.Gelu_apprx_tanh
+
+P = 128
+PACK = 4
+PASSES = K // (P * PACK)
+BLOCKS = N // P
+CHUNK = 512
+SLICE = 512
+FULL = 8
+V_SHARE = 64
+
+
+def interleave(copy, dst, src):
+    copy(
+        out=dst.rearrange("p (c i) t -> p c t i", i=4),
+        in_=src.rearrange("p t (c i) -> p c t i", i=4),
+    )
+
+
+def interleave_w(copy, dst, src):
+    copy(
+        out=dst.rearrange("p g (c i) t -> p g c t i", i=4),
+        in_=src.rearrange("p g t (c i) -> p g c t i", i=4),
+    )
+
+
+def tile_routed_moe_kernel(tc, xT, w, b, gate, offs, pos1, pos2, out):
+    nc = tc.nc
+    with ExitStack() as ctx:
+        keep = ctx.enter_context(tc.tile_pool(name="keep", bufs=1))
+        raw_pool = ctx.enter_context(tc.tile_pool(name="raw", bufs=7))
+        rawh_pool = ctx.enter_context(tc.tile_pool(name="rawh", bufs=8))
+        xb_pool = ctx.enter_context(tc.tile_pool(name="xb", bufs=4))
+        wb_pool = ctx.enter_context(tc.tile_pool(name="wb", bufs=5))
+        wc_pool = ctx.enter_context(tc.tile_pool(name="wc", bufs=4))
+        psum = ctx.enter_context(tc.psum_pool(name="psum", bufs=8))
+
+        offs_sb = keep.tile([P, E * C // 16], U16, name="offs_sb")
+        pos_sb = [keep.tile([P, T // 16], U16, name=f"pos_sb{r}") for r in range(2)]
+        bias = keep.tile([P, BLOCKS, E], F32, name="bias")
+        warm = keep.tile([P, 1], F32, name="warm")
+        xw = [keep.tile([P, T], U32, name=f"xw{g}", align_bytes=64) for g in range(PASSES)]
+        xs = keep.tile([P, T], U8, name="xs", align_bytes=64)
+        gw, gs = {}, {}
+        codes_pool = ctx.enter_context(tc.tile_pool(name="codes", bufs=3))
+        y = [keep.tile([P, E * C], F32, name=f"y{h}") for h in range(BLOCKS)]
+        gate_sb = [[keep.tile([P, T], F32, name=f"gate{h}_{r}") for r in range(2)] for h in range(BLOCKS)]
+        prod = [[keep.tile([P, T], F32, name=f"prod{h}_{r}") for r in range(2)] for h in range(BLOCKS)]
+
+        nc.gpsimd.memset(xs[:], 0)
+        nc.vector.memset(warm[:], 0.0)
+        nc.scalar.activation(out=warm[:], in_=warm[:], func=GELU)
+
+        xv = xT.rearrange("(g p t) n -> g p t n", p=P, t=PACK)
+        for g in range(PASSES):
+            for c in range(T // CHUNK):
+                raw = raw_pool.tile([P, PACK, CHUNK], F32, name="raw")
+                nc.sync.dma_start(out=raw[:], in_=xv[g, :, :, c * CHUNK : (c + 1) * CHUNK])
+                if g == 0 and c == 1:
+                    nc.sync.dma_start(offs_sb[:], offs)
+                xb = xb_pool.tile([P, CHUNK, PACK], BF16, name="xb", align_bytes=64)
+                half = CHUNK // 2
+                interleave(nc.vector.tensor_copy, xb[:, :half, :], raw[:, :, :half])
+                interleave(nc.scalar.copy, xb[:, half:, :], raw[:, :, half:])
+                nc.vector.quantize_mx(
+                    out=xw[g][:, c * CHUNK : (c + 1) * CHUNK].bitcast(FP8X4),
+                    scales=xs[4 * g : P, c * CHUNK : (c + 1) * CHUNK],
+                    in_=xb[:].rearrange("p n t -> p (n t)"),
+                )
+
+        def gather(s):
+            entries = offs_sb[:, s * SLICE // 16 : (s + 1) * SLICE // 16]
+            gw[s] = codes_pool.tile([P, PASSES, SLICE], U32, name="gw", align_bytes=64)
+            gs[s] = codes_pool.tile([P, SLICE], U8, name="gs", align_bytes=64)
+            for g in range(PASSES):
+                nc.vector.tensor_copy(gw[s][:, g, :], xw[g][:].indirect(entries))
+            nc.vector.tensor_copy(gs[s][:], xs[:].indirect(entries))
+
+        def multiply(acc, wc, ws, e, col, width, wcol):
+            s, j = e * C // SLICE, e * C % SLICE
+            for g in range(PASSES):
+                nc.tensor.matmul_mx(
+                    out=acc[:, col : col + P],
+                    lhsT=wc[:, g * width + wcol : g * width + wcol + P].bitcast(FP8X4),
+                    lhsT_scale=ws[:, g * width + wcol : g * width + wcol + P],
+                    rhs=gw[s][:, g, j : j + C].bitcast(FP8X4),
+                    rhs_scale=gs[s][4 * g : P, j : j + C],
+                    start=(g == 0),
+                    stop=(g == PASSES - 1),
+                )
+
+        def combine(h, pieces):
+            n = T // pieces
+            for q in range(pieces):
+                cols = slice(q * n, (q + 1) * n)
+                for r in range(2):
+                    nc.vector.tensor_tensor(
+                        prod[h][r][:, cols],
+                        y[h][:].indirect(pos_sb[r][:, q * n // 16 : (q + 1) * n // 16]),
+                        gate_sb[h][r][:, cols],
+                        MULT,
+                    )
+                nc.vector.tensor_tensor(prod[h][0][:, cols], prod[h][0][:, cols], prod[h][1][:, cols], ADD)
+                queue = nc.gpsimd if h == 0 else nc.sync
+                queue.dma_start(out=out[h * P : (h + 1) * P, cols], in_=prod[h][0][:, cols])
+
+        def load_gate(h):
+            for r in range(2):
+                nc.sync.dma_start(out=gate_sb[h][r][:], in_=gate[r, h * P : (h + 1) * P, :])
+
+        for e in range(FULL):
+            raw = raw_pool.tile([P, PASSES, PACK, N], F32, name="raw")
+            nc.sync.dma_start(
+                out=raw[:].rearrange("p g t n -> p g (t n)"),
+                in_=w[e].rearrange("(g p t) n -> p g (t n)", p=P, t=PACK),
+            )
+            if e == 0:
+                nc.sync.dma_start(out=bias[:], in_=b.rearrange("(h p) e -> p h e", p=P))
+                for r, pos in enumerate((pos1, pos2)):
+                    nc.sync.dma_start(pos_sb[r][:], pos)
+            if e * C % SLICE == 0:
+                gather(e * C // SLICE)
+            wb = wb_pool.tile([P, PASSES, N, PACK], BF16, name="wb", align_bytes=64)
+            cut = N - V_SHARE
+            interleave_w(nc.scalar.copy, wb[:, :, :cut, :], raw[:, :, :, :cut])
+            interleave_w(nc.vector.tensor_copy, wb[:, :, cut:, :], raw[:, :, :, cut:])
+            wc = wc_pool.tile([P, PASSES * N], U32, name="wc", align_bytes=64)
+            ws = wc_pool.tile([P, PASSES * N], U8, name="ws", align_bytes=64)
+            nc.vector.quantize_mx(out=wc[:].bitcast(FP8X4), scales=ws[:], in_=wb[:].rearrange("p g n t -> p (g n t)"))
+            acc = psum.tile([P, N], F32, name="acc")
+            for h in range(BLOCKS):
+                multiply(acc, wc, ws, e, h * P, N, h * P)
+            for h in range(BLOCKS):
+                nc.scalar.activation(
+                    out=y[h][:, e * C : (e + 1) * C], in_=acc[:, h * P : (h + 1) * P], func=GELU, bias=bias[:, h, e : e + 1]
+                )
+
+        for h in range(BLOCKS):
+            for e in range(FULL, E):
+                raw = rawh_pool.tile([P, PASSES, PACK, P], F32, name="rawh")
+                wv = w[e].rearrange("(g p t) n -> g p t n", p=P, t=PACK)
+                for g in range(PASSES):
+                    nc.sync.dma_start(out=raw[:, g, :, :], in_=wv[g, :, :, h * P : (h + 1) * P])
+                if e == E - 1 and h == 0:
+                    load_gate(0)
+                if h == 0 and e * C % SLICE == 0:
+                    gather(e * C // SLICE)
+                wb = wb_pool.tile([P, PASSES, P, PACK], BF16, name="wbh", align_bytes=64)
+                cut = 64
+                interleave_w(nc.scalar.copy, wb[:, :, :cut, :], raw[:, :, :, :cut])
+                interleave_w(nc.vector.tensor_copy, wb[:, :, cut:, :], raw[:, :, :, cut:])
+                wc = wc_pool.tile([P, PASSES * P], U32, name="wch", align_bytes=64)
+                ws = wc_pool.tile([P, PASSES * P], U8, name="wsh", align_bytes=64)
+                nc.vector.quantize_mx(out=wc[:].bitcast(FP8X4), scales=ws[:], in_=wb[:].rearrange("p g n t -> p (g n t)"))
+                acc = psum.tile([P, N], F32, name="acc")
+                multiply(acc, wc, ws, e, 0, P, 0)
+                nc.scalar.activation(
+                    out=y[h][:, e * C : (e + 1) * C], in_=acc[:, :P], func=GELU, bias=bias[:, h, e : e + 1]
+                )
+            if h == BLOCKS - 1:
+                load_gate(h)
+            combine(h, 1 if h == 0 else 2)

@@ -21,18 +21,11 @@ PASSES = K // (P * PACK)
 BLOCKS = N // P
 CHUNK = 512
 SLICE = 512
-FULL = 8
-V_SHARE = 64
+GROUP = 4
+PLAN = [("x", 0, 0, 0.25), ("w", 0, 0.5), ("x", 0, 1, 1), ("w", 1, 0), ("x", 1, 0, 0.25), ("x", 1, 1, 0.5), ("w", 2, 0.25), ("w", 3, 0), ("w", 4, 0), ("w", 5, 0), ("w", 6, 0), ("w", 7, 1), ("w", 8, 0), ("w", 9, 1), ("w", 10, 0.75), ("w", 11, 0.5), ("h", 0, 12, 0.25), ("g", 0, 0), ("h", 0, 14, 0.5), ("c", 0, 0), ("h", 1, 12, 0), ("h", 1, 14, 0), ("g", 1, 0), ("c", 1, 0)]
 
 
 def interleave(copy, dst, src):
-    copy(
-        out=dst.rearrange("p (c i) t -> p c t i", i=4),
-        in_=src.rearrange("p t (c i) -> p c t i", i=4),
-    )
-
-
-def interleave_w(copy, dst, src):
     copy(
         out=dst.rearrange("p g (c i) t -> p g c t i", i=4),
         in_=src.rearrange("p g t (c i) -> p g c t i", i=4),
@@ -43,11 +36,10 @@ def tile_routed_moe_kernel(tc, xT, w, b, gate, offs, pos1, pos2, out):
     nc = tc.nc
     with ExitStack() as ctx:
         keep = ctx.enter_context(tc.tile_pool(name="keep", bufs=1))
-        raw_pool = ctx.enter_context(tc.tile_pool(name="raw", bufs=7))
-        rawh_pool = ctx.enter_context(tc.tile_pool(name="rawh", bufs=8))
-        xb_pool = ctx.enter_context(tc.tile_pool(name="xb", bufs=4))
-        wb_pool = ctx.enter_context(tc.tile_pool(name="wb", bufs=5))
-        wc_pool = ctx.enter_context(tc.tile_pool(name="wc", bufs=4))
+        raw_pool = ctx.enter_context(tc.tile_pool(name="raw", bufs=6))
+        grouped_pool = ctx.enter_context(tc.tile_pool(name="grouped", bufs=9))
+        slots_pool = ctx.enter_context(tc.tile_pool(name="slots", bufs=2))
+        prod_pool = ctx.enter_context(tc.tile_pool(name="prod", bufs=3))
         psum = ctx.enter_context(tc.psum_pool(name="psum", bufs=8))
 
         offs_sb = keep.tile([P, E * C // 16], U16, name="offs_sb")
@@ -56,122 +48,136 @@ def tile_routed_moe_kernel(tc, xT, w, b, gate, offs, pos1, pos2, out):
         warm = keep.tile([P, 1], F32, name="warm")
         xw = [keep.tile([P, T], U32, name=f"xw{g}", align_bytes=64) for g in range(PASSES)]
         xs = keep.tile([P, T], U8, name="xs", align_bytes=64)
-        gw, gs = {}, {}
-        codes_pool = ctx.enter_context(tc.tile_pool(name="codes", bufs=3))
         y = [keep.tile([P, E * C], F32, name=f"y{h}") for h in range(BLOCKS)]
-        gate_sb = [[keep.tile([P, T], F32, name=f"gate{h}_{r}") for r in range(2)] for h in range(BLOCKS)]
-        prod = [[keep.tile([P, T], F32, name=f"prod{h}_{r}") for r in range(2)] for h in range(BLOCKS)]
+        gw, gs, pairs, waiting, bank = {}, {}, {}, [], []
 
         nc.gpsimd.memset(xs[:], 0)
         nc.vector.memset(warm[:], 0.0)
         nc.scalar.activation(out=warm[:], in_=warm[:], func=GELU)
 
         xv = xT.rearrange("(g p t) n -> g p t n", p=P, t=PACK)
-        for g in range(PASSES):
-            for c in range(T // CHUNK):
-                raw = raw_pool.tile([P, PACK, CHUNK], F32, name="raw")
-                nc.sync.dma_start(out=raw[:], in_=xv[g, :, :, c * CHUNK : (c + 1) * CHUNK])
-                if g == 0 and c == 1:
-                    nc.sync.dma_start(offs_sb[:], offs)
-                xb = xb_pool.tile([P, CHUNK, PACK], BF16, name="xb", align_bytes=64)
-                half = CHUNK // 2
-                interleave(nc.vector.tensor_copy, xb[:, :half, :], raw[:, :, :half])
-                interleave(nc.scalar.copy, xb[:, half:, :], raw[:, :, half:])
-                nc.vector.quantize_mx(
-                    out=xw[g][:, c * CHUNK : (c + 1) * CHUNK].bitcast(FP8X4),
-                    scales=xs[4 * g : P, c * CHUNK : (c + 1) * CHUNK],
-                    in_=xb[:].rearrange("p n t -> p (n t)"),
-                )
+
+        def split(dst, src, share):
+            n = dst.shape[2]
+            cut = n - int(n * share)
+            if cut > 0:
+                interleave(nc.scalar.copy, dst[:, :, :cut, :], src[:, :, :, :cut])
+            if cut < n:
+                interleave(nc.vector.tensor_copy, dst[:, :, cut:, :], src[:, :, :, cut:])
 
         def gather(s):
             entries = offs_sb[:, s * SLICE // 16 : (s + 1) * SLICE // 16]
-            gw[s] = codes_pool.tile([P, PASSES, SLICE], U32, name="gw", align_bytes=64)
-            gs[s] = codes_pool.tile([P, SLICE], U8, name="gs", align_bytes=64)
+            gw[s] = slots_pool.tile([P, PASSES, SLICE], U32, name="gw", align_bytes=64)
+            gs[s] = slots_pool.tile([P, SLICE], U8, name="gs", align_bytes=64)
             for g in range(PASSES):
                 nc.vector.tensor_copy(gw[s][:, g, :], xw[g][:].indirect(entries))
             nc.vector.tensor_copy(gs[s][:], xs[:].indirect(entries))
 
-        def multiply(acc, wc, ws, e, col, width, wcol):
+        def activate():
+            for i, (e, h, acc) in enumerate(bank):
+                nc.scalar.activation(
+                    out=y[h][:, e * C : (e + 1) * C], in_=acc[:, i * C : (i + 1) * C], func=GELU, bias=bias[:, h, e : e + 1]
+                )
+            bank.clear()
+
+        def multiply(e, h, codes, scales, width, col):
             s, j = e * C // SLICE, e * C % SLICE
+            if s not in gw:
+                gather(s)
+            acc = bank[0][2] if bank else psum.tile([P, GROUP * C], F32, name="acc")
+            i = len(bank)
+            bank.append((e, h, acc))
             for g in range(PASSES):
+                at = slice(g * width + col, g * width + col + P)
                 nc.tensor.matmul_mx(
-                    out=acc[:, col : col + P],
-                    lhsT=wc[:, g * width + wcol : g * width + wcol + P].bitcast(FP8X4),
-                    lhsT_scale=ws[:, g * width + wcol : g * width + wcol + P],
+                    out=acc[:, i * C : (i + 1) * C],
+                    lhsT=codes[:, at].bitcast(FP8X4),
+                    lhsT_scale=scales[:, at],
                     rhs=gw[s][:, g, j : j + C].bitcast(FP8X4),
                     rhs_scale=gs[s][4 * g : P, j : j + C],
                     start=(g == 0),
                     stop=(g == PASSES - 1),
                 )
+            if len(bank) == GROUP:
+                activate()
 
-        def combine(h, pieces):
+        def combine(h, pieces, queue):
             n = T // pieces
             for q in range(pieces):
                 cols = slice(q * n, (q + 1) * n)
+                prod = [prod_pool.tile([P, n], F32, name=f"prod{n}_{r}") for r in range(2)]
                 for r in range(2):
                     nc.vector.tensor_tensor(
-                        prod[h][r][:, cols],
+                        prod[r][:],
                         y[h][:].indirect(pos_sb[r][:, q * n // 16 : (q + 1) * n // 16]),
-                        gate_sb[h][r][:, cols],
+                        pairs[h][:, r, cols],
                         MULT,
                     )
-                nc.vector.tensor_tensor(prod[h][0][:, cols], prod[h][0][:, cols], prod[h][1][:, cols], ADD)
-                queue = nc.gpsimd if h == 0 else nc.sync
-                queue.dma_start(out=out[h * P : (h + 1) * P, cols], in_=prod[h][0][:, cols])
+                nc.vector.tensor_tensor(prod[0][:], prod[0][:], prod[1][:], ADD)
+                queue.dma_start(out=out[h * P : (h + 1) * P, cols], in_=prod[0][:])
 
-        def load_gate(h):
-            for r in range(2):
-                nc.sync.dma_start(out=gate_sb[h][r][:], in_=gate[r, h * P : (h + 1) * P, :])
-
-        for e in range(FULL):
-            raw = raw_pool.tile([P, PASSES, PACK, N], F32, name="raw")
-            nc.sync.dma_start(
-                out=raw[:].rearrange("p g t n -> p g (t n)"),
-                in_=w[e].rearrange("(g p t) n -> p g (t n)", p=P, t=PACK),
-            )
-            if e == 0:
+        for number, step in enumerate(PLAN):
+            kind, share = step[0], step[-1]
+            if kind == "x":
+                g, c = step[1], step[2]
+                cols = slice(c * CHUNK, (c + 1) * CHUNK)
+                raw = raw_pool.tile([P, 1, PACK, CHUNK], F32, name="raw")
+                nc.sync.dma_start(out=raw[:, 0, :, :], in_=xv[g, :, :, cols])
+                grouped = grouped_pool.tile([P, 1, CHUNK, PACK], BF16, name="grouped", align_bytes=64)
+                split(grouped, raw, share)
+                nc.vector.quantize_mx(
+                    out=xw[g][:, cols].bitcast(FP8X4),
+                    scales=xs[4 * g : P, cols],
+                    in_=grouped[:].rearrange("p g n t -> p (g n t)"),
+                )
+            elif kind == "w":
+                e = step[1]
+                raw = raw_pool.tile([P, PASSES, PACK, N], F32, name="raw")
+                nc.sync.dma_start(
+                    out=raw[:].rearrange("p g t n -> p g (t n)"),
+                    in_=w[e].rearrange("(g p t) n -> p g (t n)", p=P, t=PACK),
+                )
+                grouped = grouped_pool.tile([P, PASSES, N, PACK], BF16, name="grouped", align_bytes=64)
+                split(grouped, raw, share)
+                codes = keep.tile([P, PASSES * N], U32, name=f"codes{e}", align_bytes=64)
+                scales = keep.tile([P, PASSES * N], U8, name=f"scales{e}", align_bytes=64)
+                nc.vector.quantize_mx(out=codes[:].bitcast(FP8X4), scales=scales[:], in_=grouped[:].rearrange("p g n t -> p (g n t)"))
+                waiting.append((e, codes, scales))
+                if number >= 6:
+                    for e, codes, scales in waiting:
+                        for h in range(BLOCKS):
+                            multiply(e, h, codes, scales, N, h * P)
+                    waiting.clear()
+            elif kind == "h":
+                h, first = step[1], step[2]
+                raw = raw_pool.tile([P, 2, PASSES, PACK, P], F32, name="raw")
+                grouped = grouped_pool.tile([P, 2, PASSES, P, PACK], BF16, name="grouped", align_bytes=64)
+                for i in range(2):
+                    e = first + i
+                    for g in range(PASSES):
+                        nc.sync.dma_start(
+                            out=raw[:, i, g, :, :],
+                            in_=w[e].rearrange("(g p t) n -> g p t n", p=P, t=PACK)[g, :, :, h * P : (h + 1) * P],
+                        )
+                    part = share if share != 0.5 else i
+                    split(grouped[:, i, :, :, :], raw[:, i, :, :, :], part)
+                    codes = keep.tile([P, PASSES * P], U32, name=f"codes{h}_{e}", align_bytes=64)
+                    scales = keep.tile([P, PASSES * P], U8, name=f"scales{h}_{e}", align_bytes=64)
+                    nc.vector.quantize_mx(
+                        out=codes[:].bitcast(FP8X4), scales=scales[:], in_=grouped[:, i, :, :, :].rearrange("p g n t -> p (g n t)")
+                    )
+                    multiply(e, h, codes, scales, P, 0)
+            elif kind == "g":
+                h = step[1]
+                pairs[h] = raw_pool.tile([P, 2, T], F32, name="raw")
+                nc.sync.dma_start(out=pairs[h][:], in_=gate[:, h * P : (h + 1) * P, :].rearrange("r p n -> p r n"))
+            else:
+                h = step[1]
+                activate()
+                combine(h, 1 if h == 0 else 2, nc.gpsimd if h == 0 else nc.sync)
+            if number == 1:
+                nc.sync.dma_start(offs_sb[:], offs)
+            if number == 5:
                 nc.sync.dma_start(out=bias[:], in_=b.rearrange("(h p) e -> p h e", p=P))
                 for r, pos in enumerate((pos1, pos2)):
                     nc.sync.dma_start(pos_sb[r][:], pos)
-            if e * C % SLICE == 0:
-                gather(e * C // SLICE)
-            wb = wb_pool.tile([P, PASSES, N, PACK], BF16, name="wb", align_bytes=64)
-            cut = N - V_SHARE
-            interleave_w(nc.scalar.copy, wb[:, :, :cut, :], raw[:, :, :, :cut])
-            interleave_w(nc.vector.tensor_copy, wb[:, :, cut:, :], raw[:, :, :, cut:])
-            wc = wc_pool.tile([P, PASSES * N], U32, name="wc", align_bytes=64)
-            ws = wc_pool.tile([P, PASSES * N], U8, name="ws", align_bytes=64)
-            nc.vector.quantize_mx(out=wc[:].bitcast(FP8X4), scales=ws[:], in_=wb[:].rearrange("p g n t -> p (g n t)"))
-            acc = psum.tile([P, N], F32, name="acc")
-            for h in range(BLOCKS):
-                multiply(acc, wc, ws, e, h * P, N, h * P)
-            for h in range(BLOCKS):
-                nc.scalar.activation(
-                    out=y[h][:, e * C : (e + 1) * C], in_=acc[:, h * P : (h + 1) * P], func=GELU, bias=bias[:, h, e : e + 1]
-                )
-
-        for h in range(BLOCKS):
-            for e in range(FULL, E):
-                raw = rawh_pool.tile([P, PASSES, PACK, P], F32, name="rawh")
-                wv = w[e].rearrange("(g p t) n -> g p t n", p=P, t=PACK)
-                for g in range(PASSES):
-                    nc.sync.dma_start(out=raw[:, g, :, :], in_=wv[g, :, :, h * P : (h + 1) * P])
-                if e == E - 1 and h == 0:
-                    load_gate(0)
-                if h == 0 and e * C % SLICE == 0:
-                    gather(e * C // SLICE)
-                wb = wb_pool.tile([P, PASSES, P, PACK], BF16, name="wbh", align_bytes=64)
-                cut = 64
-                interleave_w(nc.scalar.copy, wb[:, :, :cut, :], raw[:, :, :, :cut])
-                interleave_w(nc.vector.tensor_copy, wb[:, :, cut:, :], raw[:, :, :, cut:])
-                wc = wc_pool.tile([P, PASSES * P], U32, name="wch", align_bytes=64)
-                ws = wc_pool.tile([P, PASSES * P], U8, name="wsh", align_bytes=64)
-                nc.vector.quantize_mx(out=wc[:].bitcast(FP8X4), scales=ws[:], in_=wb[:].rearrange("p g n t -> p (g n t)"))
-                acc = psum.tile([P, N], F32, name="acc")
-                multiply(acc, wc, ws, e, 0, P, 0)
-                nc.scalar.activation(
-                    out=y[h][:, e * C : (e + 1) * C], in_=acc[:, :P], func=GELU, bias=bias[:, h, e : e + 1]
-                )
-            if h == BLOCKS - 1:
-                load_gate(h)
-            combine(h, 1 if h == 0 else 2)

@@ -19,10 +19,42 @@ P = 128
 PACK = 4
 PASSES = K // (P * PACK)
 BLOCKS = N // P
-CHUNK = 512
-SLICE = 512
+SLICES = [(0, 512), (512, 512), (1024, 640), (1664, 384)]
 GROUP = 4
-PLAN = [("x", 0, 0, 0.25), ("w", 0, 0.5), ("x", 0, 1, 1), ("w", 1, 0), ("x", 1, 0, 0.25), ("x", 1, 1, 0.5), ("w", 2, 0.25), ("w", 3, 0), ("w", 4, 0), ("w", 5, 0), ("w", 6, 0), ("w", 7, 1), ("w", 8, 0), ("w", 9, 1), ("w", 10, 0.75), ("w", 11, 0.5), ("h", 0, 12, 0.25), ("g", 0, 0), ("h", 0, 14, 0.5), ("c", 0, 0), ("h", 1, 12, 0), ("h", 1, 14, 0), ("g", 1, 0), ("c", 1, 0)]
+GROUP_1 = 4
+PLAN = [
+    ("x", 0, 0, 512, 0.75),
+    ("x", 0, 512, 512, 0.75),
+    ("x", 1, 0, 512, 0),
+    ("x", 1, 512, 512, 0.5),
+    ("w", 0, 0),
+    ("w", 1, 0),
+    ("w", 2, 0),
+    ("w", 3, 1),
+    ("w", 4, 0.5),
+    ("w", 5, 0),
+    ("w", 6, 0),
+    ("w", 7, 1),
+    ("w", 8, 0.5),
+    ("w", 9, 0),
+    ("h", 0, 10, 1, 0),
+    ("h", 0, 11, 1, 0.25),
+    ("h", 0, 12, 1, 1),
+    ("h", 0, 13, 1, 0.5),
+    ("h", 0, 14, 1, 0),
+    ("h", 0, 15, 1, 1),
+    ("g", 0, 0),
+    ("c", 0, 0),
+    ("h", 1, 10, 1, 0),
+    ("h", 1, 11, 1, 0),
+    ("h", 1, 12, 1, 0),
+    ("h", 1, 13, 1, 0),
+    ("h", 1, 14, 1, 0.5),
+    ("h", 1, 15, 1, 0),
+    ("g", 1, 0),
+    ("c", 1, 0),
+]
+LAST_X = max(i for i, step in enumerate(PLAN) if step[0] == "x")
 
 
 def interleave(copy, dst, src):
@@ -36,10 +68,10 @@ def tile_routed_moe_kernel(tc, xT, w, b, gate, offs, pos1, pos2, out):
     nc = tc.nc
     with ExitStack() as ctx:
         keep = ctx.enter_context(tc.tile_pool(name="keep", bufs=1))
-        raw_pool = ctx.enter_context(tc.tile_pool(name="raw", bufs=6))
-        grouped_pool = ctx.enter_context(tc.tile_pool(name="grouped", bufs=9))
+        raw_pool = ctx.enter_context(tc.tile_pool(name="raw", bufs=9))
+        grouped_pool = ctx.enter_context(tc.tile_pool(name="grouped", bufs=7))
         slots_pool = ctx.enter_context(tc.tile_pool(name="slots", bufs=2))
-        prod_pool = ctx.enter_context(tc.tile_pool(name="prod", bufs=3))
+        prod_pool = ctx.enter_context(tc.tile_pool(name="prod", bufs=1))
         psum = ctx.enter_context(tc.psum_pool(name="psum", bufs=8))
 
         offs_sb = keep.tile([P, E * C // 16], U16, name="offs_sb")
@@ -66,9 +98,10 @@ def tile_routed_moe_kernel(tc, xT, w, b, gate, offs, pos1, pos2, out):
                 interleave(nc.vector.tensor_copy, dst[:, :, cut:, :], src[:, :, :, cut:])
 
         def gather(s):
-            entries = offs_sb[:, s * SLICE // 16 : (s + 1) * SLICE // 16]
-            gw[s] = slots_pool.tile([P, PASSES, SLICE], U32, name="gw", align_bytes=64)
-            gs[s] = slots_pool.tile([P, SLICE], U8, name="gs", align_bytes=64)
+            start, size = SLICES[s]
+            entries = offs_sb[:, start // 16 : (start + size) // 16]
+            gw[s] = slots_pool.tile([P, PASSES, size], U32, name="gw", align_bytes=64)
+            gs[s] = slots_pool.tile([P, size], U8, name="gs", align_bytes=64)
             for g in range(PASSES):
                 nc.vector.tensor_copy(gw[s][:, g, :], xw[g][:].indirect(entries))
             nc.vector.tensor_copy(gs[s][:], xs[:].indirect(entries))
@@ -80,11 +113,12 @@ def tile_routed_moe_kernel(tc, xT, w, b, gate, offs, pos1, pos2, out):
                 )
             bank.clear()
 
-        def multiply(e, h, codes, scales, width, col):
-            s, j = e * C // SLICE, e * C % SLICE
+        def multiply(e, h, codes, scales, width, col, group):
+            s = max(i for i, part in enumerate(SLICES) if part[0] <= e * C)
+            j = e * C - SLICES[s][0]
             if s not in gw:
                 gather(s)
-            acc = bank[0][2] if bank else psum.tile([P, GROUP * C], F32, name="acc")
+            acc = bank[0][2] if bank else psum.tile([P, 4 * C], F32, name="acc")
             i = len(bank)
             bank.append((e, h, acc))
             for g in range(PASSES):
@@ -98,32 +132,33 @@ def tile_routed_moe_kernel(tc, xT, w, b, gate, offs, pos1, pos2, out):
                     start=(g == 0),
                     stop=(g == PASSES - 1),
                 )
-            if len(bank) == GROUP:
+            if len(bank) == group:
                 activate()
 
-        def combine(h, pieces, queue):
-            n = T // pieces
-            for q in range(pieces):
-                cols = slice(q * n, (q + 1) * n)
-                prod = [prod_pool.tile([P, n], F32, name=f"prod{n}_{r}") for r in range(2)]
+        def combine(h, widths, queue):
+            done = 0
+            for n in widths:
+                cols = slice(done, done + n)
+                prod = [prod_pool.tile([P, n], F32, name=f"prod{h}_{n}_{r}") for r in range(2)]
                 for r in range(2):
                     nc.vector.tensor_tensor(
                         prod[r][:],
-                        y[h][:].indirect(pos_sb[r][:, q * n // 16 : (q + 1) * n // 16]),
+                        y[h][:].indirect(pos_sb[r][:, done // 16 : (done + n) // 16]),
                         pairs[h][:, r, cols],
                         MULT,
                     )
                 nc.vector.tensor_tensor(prod[0][:], prod[0][:], prod[1][:], ADD)
                 queue.dma_start(out=out[h * P : (h + 1) * P, cols], in_=prod[0][:])
+                done += n
 
         for number, step in enumerate(PLAN):
             kind, share = step[0], step[-1]
             if kind == "x":
-                g, c = step[1], step[2]
-                cols = slice(c * CHUNK, (c + 1) * CHUNK)
-                raw = raw_pool.tile([P, 1, PACK, CHUNK], F32, name="raw")
+                g, c, size = step[1], step[2], step[3]
+                cols = slice(c, c + size)
+                raw = raw_pool.tile([P, 1, PACK, size], F32, name="raw")
                 nc.sync.dma_start(out=raw[:, 0, :, :], in_=xv[g, :, :, cols])
-                grouped = grouped_pool.tile([P, 1, CHUNK, PACK], BF16, name="grouped", align_bytes=64)
+                grouped = grouped_pool.tile([P, 1, size, PACK], BF16, name="grouped", align_bytes=64)
                 split(grouped, raw, share)
                 nc.vector.quantize_mx(
                     out=xw[g][:, cols].bitcast(FP8X4),
@@ -143,30 +178,30 @@ def tile_routed_moe_kernel(tc, xT, w, b, gate, offs, pos1, pos2, out):
                 scales = keep.tile([P, PASSES * N], U8, name=f"scales{e}", align_bytes=64)
                 nc.vector.quantize_mx(out=codes[:].bitcast(FP8X4), scales=scales[:], in_=grouped[:].rearrange("p g n t -> p (g n t)"))
                 waiting.append((e, codes, scales))
-                if number >= 6:
+                if number > LAST_X:
                     for e, codes, scales in waiting:
                         for h in range(BLOCKS):
-                            multiply(e, h, codes, scales, N, h * P)
+                            multiply(e, h, codes, scales, N, h * P, GROUP)
                     waiting.clear()
             elif kind == "h":
-                h, first = step[1], step[2]
-                raw = raw_pool.tile([P, 2, PASSES, PACK, P], F32, name="raw")
-                grouped = grouped_pool.tile([P, 2, PASSES, P, PACK], BF16, name="grouped", align_bytes=64)
-                for i in range(2):
+                h, first, count = step[1], step[2], step[3]
+                raw = raw_pool.tile([P, count, PASSES, PACK, P], F32, name="raw")
+                grouped = grouped_pool.tile([P, count, PASSES, P, PACK], BF16, name="grouped", align_bytes=64)
+                for i in range(count):
                     e = first + i
                     for g in range(PASSES):
                         nc.sync.dma_start(
                             out=raw[:, i, g, :, :],
                             in_=w[e].rearrange("(g p t) n -> g p t n", p=P, t=PACK)[g, :, :, h * P : (h + 1) * P],
                         )
-                    part = share if share != 0.5 else i
+                    part = i if count == 2 and share == 0.5 else share
                     split(grouped[:, i, :, :, :], raw[:, i, :, :, :], part)
                     codes = keep.tile([P, PASSES * P], U32, name=f"codes{h}_{e}", align_bytes=64)
                     scales = keep.tile([P, PASSES * P], U8, name=f"scales{h}_{e}", align_bytes=64)
                     nc.vector.quantize_mx(
                         out=codes[:].bitcast(FP8X4), scales=scales[:], in_=grouped[:, i, :, :, :].rearrange("p g n t -> p (g n t)")
                     )
-                    multiply(e, h, codes, scales, P, 0)
+                    multiply(e, h, codes, scales, P, 0, GROUP if h == 0 else GROUP_1)
             elif kind == "g":
                 h = step[1]
                 pairs[h] = raw_pool.tile([P, 2, T], F32, name="raw")
@@ -174,10 +209,10 @@ def tile_routed_moe_kernel(tc, xT, w, b, gate, offs, pos1, pos2, out):
             else:
                 h = step[1]
                 activate()
-                combine(h, 1 if h == 0 else 2, nc.gpsimd if h == 0 else nc.sync)
+                combine(h, (1024,) if h == 0 else (768, 256,), nc.gpsimd if h == 0 else nc.sync)
             if number == 1:
                 nc.sync.dma_start(offs_sb[:], offs)
-            if number == 5:
+            if number == LAST_X:
                 nc.sync.dma_start(out=bias[:], in_=b.rearrange("(h p) e -> p h e", p=P))
                 for r, pos in enumerate((pos1, pos2)):
                     nc.sync.dma_start(pos_sb[r][:], pos)

@@ -19,40 +19,43 @@ P = 128
 PACK = 4
 PASSES = K // (P * PACK)
 BLOCKS = N // P
-SLICES = [(0, 512), (512, 512), (1024, 640), (1664, 384)]
-GROUP = 4
-GROUP_1 = 4
+SLICES = [(0, 512), (512, 512), (1024, 512), (1536, 512)]
+GROUP = 8
+LANES = 2
+PIECES = ((1024,), (768, 256,))
 PLAN = [
-    ("x", 0, 0, 512, 0.75),
-    ("x", 0, 512, 512, 0.75),
-    ("x", 1, 0, 512, 0),
-    ("x", 1, 512, 512, 0.5),
-    ("w", 0, 0),
-    ("w", 1, 0),
-    ("w", 2, 0),
-    ("w", 3, 1),
-    ("w", 4, 0.5),
-    ("w", 5, 0),
-    ("w", 6, 0),
-    ("w", 7, 1),
-    ("w", 8, 0.5),
-    ("w", 9, 0),
-    ("h", 0, 10, 1, 0),
-    ("h", 0, 11, 1, 0.25),
-    ("h", 0, 12, 1, 1),
-    ("h", 0, 13, 1, 0.5),
-    ("h", 0, 14, 1, 0),
-    ("h", 0, 15, 1, 1),
-    ("g", 0, 0),
-    ("c", 0, 0),
-    ("h", 1, 10, 1, 0),
-    ("h", 1, 11, 1, 0),
-    ("h", 1, 12, 1, 0),
-    ("h", 1, 13, 1, 0),
-    ("h", 1, 14, 1, 0.5),
-    ("h", 1, 15, 1, 0),
-    ("g", 1, 0),
-    ("c", 1, 0),
+    ("x", 0, 0, 256, (0.25,)),
+    ("x", 0, 256, 256, (1,)),
+    ("x", 0, 512, 512, (0.75,)),
+    ("x", 1, 0, 512, (0,)),
+    ("x", 1, 512, 256, (0,)),
+    ("x", 1, 768, 256, (0.5,)),
+    ("W", 0, 1, (0.25,)),
+    ("W", 1, 1, (0,)),
+    ("W", 2, 1, (0,)),
+    ("W", 3, 1, (0,)),
+    ("W", 4, 1, (0.75,)),
+    ("W", 5, 1, (0.75,)),
+    ("W", 6, 1, (0,)),
+    ("W", 7, 1, (0,)),
+    ("H", 0, 8, 1, (0,)),
+    ("H", 0, 9, 2, (0.75, 0,)),
+    ("H", 0, 11, 1, (0,)),
+    ("H", 0, 12, 2, (0, 1,)),
+    ("g", 0, ()),
+    ("H", 0, 14, 1, (0,)),
+    ("H", 0, 15, 1, (0.5,)),
+    ("H", 1, 8, 1, (0,)),
+    ("H", 1, 9, 1, (1,)),
+    ("c", 0, ()),
+    ("H", 1, 10, 1, (0,)),
+    ("H", 1, 11, 1, (0,)),
+    ("H", 1, 12, 1, (0,)),
+    ("H", 1, 13, 1, (0,)),
+    ("H", 1, 14, 1, (0,)),
+    ("H", 1, 15, 1, (0,)),
+    ("g", 1, ()),
+    ("c", 1, ()),
 ]
 LAST_X = max(i for i, step in enumerate(PLAN) if step[0] == "x")
 
@@ -68,10 +71,12 @@ def tile_routed_moe_kernel(tc, xT, w, b, gate, offs, pos1, pos2, out):
     nc = tc.nc
     with ExitStack() as ctx:
         keep = ctx.enter_context(tc.tile_pool(name="keep", bufs=1))
-        raw_pool = ctx.enter_context(tc.tile_pool(name="raw", bufs=9))
-        grouped_pool = ctx.enter_context(tc.tile_pool(name="grouped", bufs=7))
+        raw_pool = ctx.enter_context(tc.tile_pool(name="raw", bufs=5))
+        half_pool = ctx.enter_context(tc.tile_pool(name="half", bufs=6))
+        xgrouped_pool = ctx.enter_context(tc.tile_pool(name="xgrouped", bufs=5))
+        grouped_pool = ctx.enter_context(tc.tile_pool(name="grouped", bufs=6))
         slots_pool = ctx.enter_context(tc.tile_pool(name="slots", bufs=2))
-        prod_pool = ctx.enter_context(tc.tile_pool(name="prod", bufs=1))
+        prod_pool = ctx.enter_context(tc.tile_pool(name="prod", bufs=2))
         psum = ctx.enter_context(tc.psum_pool(name="psum", bufs=8))
 
         offs_sb = keep.tile([P, E * C // 16], U16, name="offs_sb")
@@ -81,7 +86,7 @@ def tile_routed_moe_kernel(tc, xT, w, b, gate, offs, pos1, pos2, out):
         xw = [keep.tile([P, T], U32, name=f"xw{g}", align_bytes=64) for g in range(PASSES)]
         xs = keep.tile([P, T], U8, name="xs", align_bytes=64)
         y = [keep.tile([P, E * C], F32, name=f"y{h}") for h in range(BLOCKS)]
-        gw, gs, pairs, waiting, bank = {}, {}, {}, [], []
+        gw, gs, pairs, waiting, banks, members = {}, {}, {}, [], [], []
 
         nc.gpsimd.memset(xs[:], 0)
         nc.vector.memset(warm[:], 0.0)
@@ -107,24 +112,27 @@ def tile_routed_moe_kernel(tc, xT, w, b, gate, offs, pos1, pos2, out):
             nc.vector.tensor_copy(gs[s][:], xs[:].indirect(entries))
 
         def activate():
-            for i, (e, h, acc) in enumerate(bank):
+            for i, (e, h) in enumerate(members):
+                at = slice(i // LANES * C, (i // LANES + 1) * C)
                 nc.scalar.activation(
-                    out=y[h][:, e * C : (e + 1) * C], in_=acc[:, i * C : (i + 1) * C], func=GELU, bias=bias[:, h, e : e + 1]
+                    out=y[h][:, e * C : (e + 1) * C], in_=banks[i % LANES][:, at], func=GELU, bias=bias[:, h, e : e + 1]
                 )
-            bank.clear()
+            members.clear()
+            banks.clear()
 
-        def multiply(e, h, codes, scales, width, col, group):
+        def multiply(e, h, codes, scales, width, col):
             s = max(i for i, part in enumerate(SLICES) if part[0] <= e * C)
             j = e * C - SLICES[s][0]
             if s not in gw:
                 gather(s)
-            acc = bank[0][2] if bank else psum.tile([P, 4 * C], F32, name="acc")
-            i = len(bank)
-            bank.append((e, h, acc))
+            if not members:
+                banks.extend([psum.tile([P, 4 * C], F32, name="acc") for lane in range(LANES)])
+            i = len(members)
+            members.append((e, h))
             for g in range(PASSES):
                 at = slice(g * width + col, g * width + col + P)
                 nc.tensor.matmul_mx(
-                    out=acc[:, i * C : (i + 1) * C],
+                    out=banks[i % LANES][:, i // LANES * C : (i // LANES + 1) * C],
                     lhsT=codes[:, at].bitcast(FP8X4),
                     lhsT_scale=scales[:, at],
                     rhs=gw[s][:, g, j : j + C].bitcast(FP8X4),
@@ -132,12 +140,12 @@ def tile_routed_moe_kernel(tc, xT, w, b, gate, offs, pos1, pos2, out):
                     start=(g == 0),
                     stop=(g == PASSES - 1),
                 )
-            if len(bank) == group:
+            if len(members) == GROUP:
                 activate()
 
-        def combine(h, widths, queue):
+        def combine(h, queue):
             done = 0
-            for n in widths:
+            for n in PIECES[h]:
                 cols = slice(done, done + n)
                 prod = [prod_pool.tile([P, n], F32, name=f"prod{h}_{n}_{r}") for r in range(2)]
                 for r in range(2):
@@ -152,64 +160,60 @@ def tile_routed_moe_kernel(tc, xT, w, b, gate, offs, pos1, pos2, out):
                 done += n
 
         for number, step in enumerate(PLAN):
-            kind, share = step[0], step[-1]
+            kind, shares = step[0], step[-1]
             if kind == "x":
                 g, c, size = step[1], step[2], step[3]
                 cols = slice(c, c + size)
                 raw = raw_pool.tile([P, 1, PACK, size], F32, name="raw")
                 nc.sync.dma_start(out=raw[:, 0, :, :], in_=xv[g, :, :, cols])
-                grouped = grouped_pool.tile([P, 1, size, PACK], BF16, name="grouped", align_bytes=64)
-                split(grouped, raw, share)
+                grouped = xgrouped_pool.tile([P, 1, size, PACK], BF16, name="xgrouped", align_bytes=64)
+                split(grouped, raw, shares[0])
                 nc.vector.quantize_mx(
                     out=xw[g][:, cols].bitcast(FP8X4),
                     scales=xs[4 * g : P, cols],
                     in_=grouped[:].rearrange("p g n t -> p (g n t)"),
                 )
-            elif kind == "w":
-                e = step[1]
-                raw = raw_pool.tile([P, PASSES, PACK, N], F32, name="raw")
-                nc.sync.dma_start(
-                    out=raw[:].rearrange("p g t n -> p g (t n)"),
-                    in_=w[e].rearrange("(g p t) n -> p g (t n)", p=P, t=PACK),
-                )
-                grouped = grouped_pool.tile([P, PASSES, N, PACK], BF16, name="grouped", align_bytes=64)
-                split(grouped, raw, share)
-                codes = keep.tile([P, PASSES * N], U32, name=f"codes{e}", align_bytes=64)
-                scales = keep.tile([P, PASSES * N], U8, name=f"scales{e}", align_bytes=64)
-                nc.vector.quantize_mx(out=codes[:].bitcast(FP8X4), scales=scales[:], in_=grouped[:].rearrange("p g n t -> p (g n t)"))
-                waiting.append((e, codes, scales))
-                if number > LAST_X:
-                    for e, codes, scales in waiting:
-                        for h in range(BLOCKS):
-                            multiply(e, h, codes, scales, N, h * P, GROUP)
-                    waiting.clear()
-            elif kind == "h":
-                h, first, count = step[1], step[2], step[3]
-                raw = raw_pool.tile([P, count, PASSES, PACK, P], F32, name="raw")
-                grouped = grouped_pool.tile([P, count, PASSES, P, PACK], BF16, name="grouped", align_bytes=64)
+            elif kind == "W" or kind == "H":
+                whole = kind == "W"
+                width = N if whole else P
+                first, count = step[-3], step[-2]
+                h = 0 if whole else step[1]
+                grouped = grouped_pool.tile([P, count * PASSES, width, PACK], BF16, name="grouped", align_bytes=64)
                 for i in range(count):
-                    e = first + i
-                    for g in range(PASSES):
+                    if whole:
+                        raw = raw_pool.tile([P, PASSES, PACK, N], F32, name="raw")
                         nc.sync.dma_start(
-                            out=raw[:, i, g, :, :],
-                            in_=w[e].rearrange("(g p t) n -> g p t n", p=P, t=PACK)[g, :, :, h * P : (h + 1) * P],
+                            out=raw[:].rearrange("p g t n -> p g (t n)"),
+                            in_=w[first + i].rearrange("(g p t) n -> p g (t n)", p=P, t=PACK),
                         )
-                    part = i if count == 2 and share == 0.5 else share
-                    split(grouped[:, i, :, :, :], raw[:, i, :, :, :], part)
-                    codes = keep.tile([P, PASSES * P], U32, name=f"codes{h}_{e}", align_bytes=64)
-                    scales = keep.tile([P, PASSES * P], U8, name=f"scales{h}_{e}", align_bytes=64)
-                    nc.vector.quantize_mx(
-                        out=codes[:].bitcast(FP8X4), scales=scales[:], in_=grouped[:, i, :, :, :].rearrange("p g n t -> p (g n t)")
-                    )
-                    multiply(e, h, codes, scales, P, 0, GROUP if h == 0 else GROUP_1)
+                    else:
+                        raw = half_pool.tile([P, PASSES, PACK, P], F32, name="half")
+                        for g in range(PASSES):
+                            nc.sync.dma_start(
+                                out=raw[:, g, :, :],
+                                in_=w[first + i].rearrange("(g p t) n -> g p t n", p=P, t=PACK)[g, :, :, h * P : (h + 1) * P],
+                            )
+                    split(grouped[:, i * PASSES : (i + 1) * PASSES, :, :], raw, shares[i])
+                codes = keep.tile([P, count * PASSES * width], U32, name=f"codes{number}", align_bytes=64)
+                scales = keep.tile([P, count * PASSES * width], U8, name=f"scales{number}", align_bytes=64)
+                nc.vector.quantize_mx(out=codes[:].bitcast(FP8X4), scales=scales[:], in_=grouped[:].rearrange("p g n t -> p (g n t)"))
+                for i in range(count):
+                    part = slice(i * PASSES * width, (i + 1) * PASSES * width)
+                    for block in range(BLOCKS) if whole else (h,):
+                        waiting.append((first + i, block, codes[:, part], scales[:, part], width, block * P if whole else 0))
+                if number > LAST_X:
+                    for item in waiting:
+                        multiply(*item)
+                    waiting.clear()
             elif kind == "g":
                 h = step[1]
                 pairs[h] = raw_pool.tile([P, 2, T], F32, name="raw")
                 nc.sync.dma_start(out=pairs[h][:], in_=gate[:, h * P : (h + 1) * P, :].rearrange("r p n -> p r n"))
             else:
                 h = step[1]
-                activate()
-                combine(h, (1024,) if h == 0 else (768, 256,), nc.gpsimd if h == 0 else nc.sync)
+                if any(block == h for e, block in members):
+                    activate()
+                combine(h, nc.gpsimd if h == 0 else nc.sync)
             if number == 1:
                 nc.sync.dma_start(offs_sb[:], offs)
             if number == LAST_X:

from contextlib import ExitStack

import concourse.mybir as mybir

K, T, E, C, N = 1024, 1024, 16, 128, 256
FLOPS = 2 * K * N * E * C

F32 = mybir.dt.float32
BF16 = mybir.dt.bfloat16
U32 = mybir.dt.uint32
U16 = mybir.dt.uint16
U8 = mybir.dt.uint8
FP8X4 = mybir.dt.float8_e4m3fn_x4
MULT = mybir.AluOpType.mult
ADD = mybir.AluOpType.add
GELU = mybir.ActivationFunctionType.Gelu_apprx_tanh

P = 128
PACK = 4
PASSES = K // (P * PACK)
BLOCKS = N // P
SLICES = [(0, 512), (512, 512), (1024, 512), (1536, 512)]
GROUP = 8
LANES = 2
PIECES = ((1024,), (768, 256,))
PLAN = [
    ("x", 0, 0, 256, (0.25,)),
    ("x", 0, 256, 256, (1,)),
    ("x", 0, 512, 512, (0.75,)),
    ("x", 1, 0, 512, (0,)),
    ("x", 1, 512, 256, (0,)),
    ("x", 1, 768, 256, (0.5,)),
    ("W", 0, 1, (0.25,)),
    ("W", 1, 1, (0,)),
    ("W", 2, 1, (0,)),
    ("W", 3, 1, (0,)),
    ("W", 4, 1, (0.75,)),
    ("W", 5, 1, (0.75,)),
    ("W", 6, 1, (0,)),
    ("W", 7, 1, (0,)),
    ("H", 0, 8, 1, (0,)),
    ("H", 0, 9, 2, (0.75, 0,)),
    ("H", 0, 11, 1, (0,)),
    ("H", 0, 12, 2, (0, 1,)),
    ("g", 0, ()),
    ("H", 0, 14, 1, (0,)),
    ("H", 0, 15, 1, (0.5,)),
    ("H", 1, 8, 1, (0,)),
    ("H", 1, 9, 1, (1,)),
    ("c", 0, ()),
    ("H", 1, 10, 1, (0,)),
    ("H", 1, 11, 1, (0,)),
    ("H", 1, 12, 1, (0,)),
    ("H", 1, 13, 1, (0,)),
    ("H", 1, 14, 1, (0,)),
    ("H", 1, 15, 1, (0,)),
    ("g", 1, ()),
    ("c", 1, ()),
]
LAST_X = max(i for i, step in enumerate(PLAN) if step[0] == "x")


def interleave(copy, dst, src):
    copy(
        out=dst.rearrange("p g (c i) t -> p g c t i", i=4),
        in_=src.rearrange("p g t (c i) -> p g c t i", i=4),
    )


def tile_routed_moe_kernel(tc, xT, w, b, gate, offs, pos1, pos2, out):
    nc = tc.nc
    with ExitStack() as ctx:
        keep = ctx.enter_context(tc.tile_pool(name="keep", bufs=1))
        raw_pool = ctx.enter_context(tc.tile_pool(name="raw", bufs=5))
        half_pool = ctx.enter_context(tc.tile_pool(name="half", bufs=6))
        xgrouped_pool = ctx.enter_context(tc.tile_pool(name="xgrouped", bufs=5))
        grouped_pool = ctx.enter_context(tc.tile_pool(name="grouped", bufs=6))
        slots_pool = ctx.enter_context(tc.tile_pool(name="slots", bufs=2))
        prod_pool = ctx.enter_context(tc.tile_pool(name="prod", bufs=2))
        psum = ctx.enter_context(tc.psum_pool(name="psum", bufs=8))

        offs_sb = keep.tile([P, E * C // 16], U16, name="offs_sb")
        pos_sb = [keep.tile([P, T // 16], U16, name=f"pos_sb{r}") for r in range(2)]
        bias = keep.tile([P, BLOCKS, E], F32, name="bias")
        warm = keep.tile([P, 1], F32, name="warm")
        xw = [keep.tile([P, T], U32, name=f"xw{g}", align_bytes=64) for g in range(PASSES)]
        xs = keep.tile([P, T], U8, name="xs", align_bytes=64)
        y = [keep.tile([P, E * C], F32, name=f"y{h}") for h in range(BLOCKS)]
        gw, gs, pairs, waiting, banks, members = {}, {}, {}, [], [], []

        nc.gpsimd.memset(xs[:], 0)
        nc.vector.memset(warm[:], 0.0)
        nc.scalar.activation(out=warm[:], in_=warm[:], func=GELU)

        xv = xT.rearrange("(g p t) n -> g p t n", p=P, t=PACK)

        def split(dst, src, share):
            n = dst.shape[2]
            cut = n - int(n * share)
            if cut > 0:
                interleave(nc.scalar.copy, dst[:, :, :cut, :], src[:, :, :, :cut])
            if cut < n:
                interleave(nc.vector.tensor_copy, dst[:, :, cut:, :], src[:, :, :, cut:])

        def gather(s):
            start, size = SLICES[s]
            entries = offs_sb[:, start // 16 : (start + size) // 16]
            gw[s] = slots_pool.tile([P, PASSES, size], U32, name="gw", align_bytes=64)
            gs[s] = slots_pool.tile([P, size], U8, name="gs", align_bytes=64)
            for g in range(PASSES):
                nc.vector.tensor_copy(gw[s][:, g, :], xw[g][:].indirect(entries))
            nc.vector.tensor_copy(gs[s][:], xs[:].indirect(entries))

        def activate():
            for i, (e, h) in enumerate(members):
                at = slice(i // LANES * C, (i // LANES + 1) * C)
                nc.scalar.activation(
                    out=y[h][:, e * C : (e + 1) * C], in_=banks[i % LANES][:, at], func=GELU, bias=bias[:, h, e : e + 1]
                )
            members.clear()
            banks.clear()

        def multiply(e, h, codes, scales, width, col):
            s = max(i for i, part in enumerate(SLICES) if part[0] <= e * C)
            j = e * C - SLICES[s][0]
            if s not in gw:
                gather(s)
            if not members:
                banks.extend([psum.tile([P, 4 * C], F32, name="acc") for lane in range(LANES)])
            i = len(members)
            members.append((e, h))
            for g in range(PASSES):
                at = slice(g * width + col, g * width + col + P)
                nc.tensor.matmul_mx(
                    out=banks[i % LANES][:, i // LANES * C : (i // LANES + 1) * C],
                    lhsT=codes[:, at].bitcast(FP8X4),
                    lhsT_scale=scales[:, at],
                    rhs=gw[s][:, g, j : j + C].bitcast(FP8X4),
                    rhs_scale=gs[s][4 * g : P, j : j + C],
                    start=(g == 0),
                    stop=(g == PASSES - 1),
                )
            if len(members) == GROUP:
                activate()

        def combine(h, queue):
            done = 0
            for n in PIECES[h]:
                cols = slice(done, done + n)
                prod = [prod_pool.tile([P, n], F32, name=f"prod{h}_{n}_{r}") for r in range(2)]
                for r in range(2):
                    nc.vector.tensor_tensor(
                        prod[r][:],
                        y[h][:].indirect(pos_sb[r][:, done // 16 : (done + n) // 16]),
                        pairs[h][:, r, cols],
                        MULT,
                    )
                nc.vector.tensor_tensor(prod[0][:], prod[0][:], prod[1][:], ADD)
                queue.dma_start(out=out[h * P : (h + 1) * P, cols], in_=prod[0][:])
                done += n

        for number, step in enumerate(PLAN):
            kind, shares = step[0], step[-1]
            if kind == "x":
                g, c, size = step[1], step[2], step[3]
                cols = slice(c, c + size)
                raw = raw_pool.tile([P, 1, PACK, size], F32, name="raw")
                nc.sync.dma_start(out=raw[:, 0, :, :], in_=xv[g, :, :, cols])
                grouped = xgrouped_pool.tile([P, 1, size, PACK], BF16, name="xgrouped", align_bytes=64)
                split(grouped, raw, shares[0])
                nc.vector.quantize_mx(
                    out=xw[g][:, cols].bitcast(FP8X4),
                    scales=xs[4 * g : P, cols],
                    in_=grouped[:].rearrange("p g n t -> p (g n t)"),
                )
            elif kind == "W" or kind == "H":
                whole = kind == "W"
                width = N if whole else P
                first, count = step[-3], step[-2]
                h = 0 if whole else step[1]
                grouped = grouped_pool.tile([P, count * PASSES, width, PACK], BF16, name="grouped", align_bytes=64)
                for i in range(count):
                    if whole:
                        raw = raw_pool.tile([P, PASSES, PACK, N], F32, name="raw")
                        nc.sync.dma_start(
                            out=raw[:].rearrange("p g t n -> p g (t n)"),
                            in_=w[first + i].rearrange("(g p t) n -> p g (t n)", p=P, t=PACK),
                        )
                    else:
                        raw = half_pool.tile([P, PASSES, PACK, P], F32, name="half")
                        for g in range(PASSES):
                            nc.sync.dma_start(
                                out=raw[:, g, :, :],
                                in_=w[first + i].rearrange("(g p t) n -> g p t n", p=P, t=PACK)[g, :, :, h * P : (h + 1) * P],
                            )
                    split(grouped[:, i * PASSES : (i + 1) * PASSES, :, :], raw, shares[i])
                codes = keep.tile([P, count * PASSES * width], U32, name=f"codes{number}", align_bytes=64)
                scales = keep.tile([P, count * PASSES * width], U8, name=f"scales{number}", align_bytes=64)
                nc.vector.quantize_mx(out=codes[:].bitcast(FP8X4), scales=scales[:], in_=grouped[:].rearrange("p g n t -> p (g n t)"))
                for i in range(count):
                    part = slice(i * PASSES * width, (i + 1) * PASSES * width)
                    for block in range(BLOCKS) if whole else (h,):
                        waiting.append((first + i, block, codes[:, part], scales[:, part], width, block * P if whole else 0))
                if number > LAST_X:
                    for item in waiting:
                        multiply(*item)
                    waiting.clear()
            elif kind == "g":
                h = step[1]
                pairs[h] = raw_pool.tile([P, 2, T], F32, name="raw")
                nc.sync.dma_start(out=pairs[h][:], in_=gate[:, h * P : (h + 1) * P, :].rearrange("r p n -> p r n"))
            else:
                h = step[1]
                if any(block == h for e, block in members):
                    activate()
                combine(h, nc.gpsimd if h == 0 else nc.sync)
            if number == 1:
                nc.sync.dma_start(offs_sb[:], offs)
            if number == LAST_X:
                nc.sync.dma_start(out=bias[:], in_=b.rearrange("(h p) e -> p h e", p=P))
                for r, pos in enumerate((pos1, pos2)):
                    nc.sync.dma_start(pos_sb[r][:], pos)
